import numpy as np
import ml_dtypes


def mxq(x, axis, fmt="e4m3"):
    dtype, down = {"e4m3": (ml_dtypes.float8_e4m3fn, 7), "e5m2": (ml_dtypes.float8_e5m2, 14)}[fmt]
    v = np.moveaxis(np.asarray(x, np.float32).astype(ml_dtypes.bfloat16).astype(np.float64), axis, -1)
    blocks = v.reshape(v.shape[:-1] + (-1, 32))
    amax = np.abs(blocks).max(-1, keepdims=True)
    byte = np.maximum(np.where(amax > 0, np.frexp(amax)[1] - 1 + 127, 0) - down, 1)
    scale = np.exp2(byte - 127.0)
    codes = (blocks / scale).astype(np.float32).astype(dtype).astype(np.float64)
    return np.moveaxis((codes * scale).reshape(v.shape), -1, axis)


WIDE = False


def mx_kscale(k):
    if not WIDE:
        return np.ones(k)
    levels = np.array([30, -30])
    if k % 512:
        return np.exp2(np.random.permutation(np.resize(levels, k // 32))).repeat(32)
    a = np.empty((k // 512, 16))
    for p in range(k // 512):
        a[p, :8] = np.random.permutation(np.resize(levels, 8))
        for g in range(8):
            far = levels[np.abs(levels - a[p, g]) >= 10]
            a[p, g + 8] = far[np.random.randint(len(far))]
    return np.exp2(a.ravel()).repeat(32)


def f64(x):
    return np.asarray(x).astype(np.float64)


def striped(idx):
    return np.tile(np.asarray(idx).reshape(-1, 16).T, (8, 1)).astype(np.uint16)


def unstriped(offs):
    return offs[:16].T.reshape(-1).astype(np.int64)


E2M1 = np.array([0.0, 0.5, 1.0, 1.5, 2.0, 3.0, 4.0, 6.0, -0.0, -0.5, -1.0, -1.5, -2.0, -3.0, -4.0, -6.0])


def pack_weight(w, fmt):
    k, n = w.shape
    w = f64(np.asarray(w, np.float32).astype(ml_dtypes.bfloat16)).reshape(k // 32, 32, n)
    amax = np.abs(w).max(1)
    if fmt in ("e4m3", "e5m2"):
        byte = np.frexp(amax)[1] - 1 + 127 - (7 if fmt == "e4m3" else 14)
    else:
        mant, ex = np.frexp(amax / 6.0)
        byte = np.where(mant > 0.5, ex, ex - 1) + 127
    byte = np.clip(np.where(amax > 0, byte, 1), 1, 254)
    scaled = (w * np.exp2(127.0 - byte)[:, None, :]).reshape(k, n).astype(np.float32)
    by_word = np.ascontiguousarray(scaled.reshape(k // 512, 128, 4, n).transpose(0, 1, 3, 2))
    if fmt in ("e4m3", "e5m2"):
        words = by_word.astype(ml_dtypes.float8_e4m3fn if fmt == "e4m3" else ml_dtypes.float8_e5m2).view(np.uint8)
    else:
        c = by_word.astype(ml_dtypes.float4_e2m1fn).view(np.uint8) & 0xF
        words = (c[..., 0::2] | (c[..., 1::2] << 4)).reshape(k // 512, 128, 2 * n)
    return np.ascontiguousarray(words), np.ascontiguousarray(byte.astype(np.uint8).reshape(k // 512, 16, n))


def unpack_weight(words, scales, fmt):
    g, _, n = scales.shape
    words = np.ascontiguousarray(words).reshape(g, 128, n, -1)
    if fmt in ("e4m3", "e5m2"):
        vals = words.view(ml_dtypes.float8_e4m3fn if fmt == "e4m3" else ml_dtypes.float8_e5m2).astype(np.float64)
    else:
        nib = np.empty((g, 128, n, 4), np.uint8)
        nib[..., 0::2] = words & 0xF
        nib[..., 1::2] = words >> 4
        vals = E2M1[nib]
    vals = vals * np.repeat(np.exp2(scales.astype(np.float64) - 127.0), 8, axis=1)[..., None]
    return vals.transpose(0, 1, 3, 2).reshape(g * 512, n)


K, T, J, R, C, O, N = 512, 1024, 256, 512, 512, 128, 256


def setup_inputs():
    n = np.random.standard_normal
    idx = np.random.permutation(T)[:J]
    idx2 = np.random.permutation(C)[:J]
    idx3 = np.random.permutation(C)[:J]
    idx4 = np.random.permutation(J)[:O]
    idx5 = np.random.permutation(J)[:O]
    fk = mx_kscale(K)
    fr = mx_kscale(R)
    xtp = pack_weight(n((K, T)) / fk[:, None], "e2m1")
    wp = pack_weight(n((K, R)) * 1 / np.sqrt(K) * fk[:, None] * fr, "e4m3")
    w2p = pack_weight(n((K, R)) * 1 / np.sqrt(K) * fk[:, None] * fr, "e5m2")
    wbp = pack_weight(n((R, N)) * 1 / np.sqrt(R) / fr[:, None], "e2m1")
    return {
        "xt_words": xtp[0],
        "xt_scales": xtp[1],
        "w_words": wp[0],
        "w_scales": wp[1],
        "w2_words": w2p[0],
        "w2_scales": w2p[1],
        "sa": (np.random.uniform(0.5, 1.6, (R, 1))).astype(np.float32),
        "sb": (np.random.uniform(0.5, 1.6, (R, 1))).astype(np.float32),
        "wb_words": wbp[0],
        "wb_scales": wbp[1],
        "offs": striped(idx),
        "offs2": striped(idx2),
        "offs3": striped(idx3),
        "offs4": striped(idx4),
        "offs5": striped(idx5),
    }


def reference(xt_words, xt_scales, w_words, w_scales, w2_words, w2_scales, sa, sb, wb_words, wb_scales, offs, offs2, offs3, offs4, offs5):
    idx = unstriped(offs)
    idx2 = unstriped(offs2)
    idx3 = unstriped(offs3)
    idx4 = unstriped(offs4)
    idx5 = unstriped(offs5)
    xtu = unpack_weight(xt_words, xt_scales, "e2m1")
    wu = unpack_weight(w_words, w_scales, "e4m3")
    w2u = unpack_weight(w2_words, w2_scales, "e5m2")
    wbu = unpack_weight(wb_words, wb_scales, "e2m1")
    xtidxg = xtu[:, idx]
    a = wu.T @ xtidxg
    b = w2u.T @ xtidxg
    pw = np.zeros((R, C))
    pw[:, idx2] = a
    rb = np.maximum(pw[:, idx3] * f64(sa), b)
    hid = np.abs(rb[:, idx4] - rb[:, idx5] * f64(sb))
    hidq = mxq(hid, 0, "e5m2")
    y = wbu.T @ hidq
    return y

@@ -1,0 +1,184 @@
+from contextlib import ExitStack
+
+import concourse.mybir as mybir
+
+K, T, J, R, C, O, N = 512, 1024, 256, 512, 512, 128, 256
+FLOPS = 2 * K * R * J * 2 + 2 * R * N * O
+
+F32 = mybir.dt.float32
+BF16 = mybir.dt.bfloat16
+I32 = mybir.dt.int32
+U32 = mybir.dt.uint32
+U16 = mybir.dt.uint16
+U8 = mybir.dt.uint8
+E4M3 = mybir.dt.float8_e4m3fn_x4
+E5M2 = mybir.dt.float8_e5m2_x4
+E2M1 = mybir.dt.float4_e2m1fn_x4
+ACT = mybir.ActivationFunctionType
+ALU = mybir.AluOpType
+
+P = 128
+PACK = 4
+SCALAR_COLUMNS = 12
+
+
+def tile_list_boardanswer_twow_one_plain_kernel(
+    tc, xt_words, xt_scales, w_words, w_scales, w2_words, w2_scales, sa, sb,
+    wb_words, wb_scales, offs, offs2, offs3, offs4, offs5, out,
+):
+    nc = tc.nc
+    with ExitStack() as ctx:
+        keep = ctx.enter_context(tc.tile_pool(name="keep", bufs=1))
+        psum = ctx.enter_context(tc.psum_pool(name="psum", bufs=1))
+
+        def sbuf(name, shape, dtype):
+            return keep.tile(shape, dtype, name=name, align_bytes=64)
+
+        def load_list(name, src):
+            dst = sbuf(name, list(src.shape), U16)
+            nc.sync.dma_start(dst[:], src)
+            return dst
+
+        def zeroed_plane(engine, name, width):
+            plane = sbuf(name, [P, width], U8)
+            engine.memset(plane[:].bitcast(I32), 0)
+            return plane
+
+        def load_scale_rows(queue, plane, src, quadrant):
+            queue.dma_start(
+                plane[32 * quadrant : 32 * quadrant + 4, :].bitcast(I32),
+                src[0, 4 * quadrant : 4 * quadrant + 4, :].bitcast(I32),
+            )
+
+        def load_words(queue, name, shape, dtype, src):
+            dst = sbuf(name, shape, dtype)
+            queue.dma_start(dst[:].bitcast(I32), src.bitcast(I32))
+            return dst
+
+        def deal(copy, name, src, dtype, order):
+            dst = sbuf(name, [P, PACK, P], dtype)
+            copy(dst[:].rearrange(f"p t m -> {order}"), src[:].rearrange(f"p (m t) -> {order}", t=PACK))
+            return dst
+
+        xt_plane = zeroed_plane(nc.vector, "xt_plane", T)
+        w_plane = zeroed_plane(nc.vector, "w_plane", R)
+
+        w_rows = sbuf("w_rows", [4, 4, R // 4], I32)
+        nc.sync.dma_start(w_rows[:], w_scales[0].bitcast(I32).rearrange("(q r) c -> r q c", r=4))
+        list1 = load_list("list1", offs)
+        xt_codes = load_words(nc.scalar, "xt_codes", [P, T], U16, xt_words[0])
+        w_codes = load_words(nc.scalar, "w_codes", [P, R], U32, w_words[0].rearrange("p n t -> p (n t)"))
+        for q in range(4):
+            load_scale_rows(nc.sync, xt_plane, xt_scales, q)
+        list2 = load_list("list2", offs2)
+
+        w2_plane = zeroed_plane(nc.gpsimd, "w2_plane", R)
+        wb_plane = zeroed_plane(nc.gpsimd, "wb_plane", N)
+        boards = []
+        for t in range(PACK):
+            board = sbuf(f"board{t}", [P, C], F32)
+            (nc.vector if t % 2 == 0 else nc.gpsimd).memset(board[:], 0.0)
+            boards.append(board)
+
+        w2_codes = load_words(nc.sync, "w2_codes", [P, R], U32, w2_words[0].rearrange("p n t -> p (n t)"))
+        for q in range(4):
+            load_scale_rows(nc.sync, w2_plane, w2_scales, q)
+        list3 = load_list("list3", offs3)
+        sa_t = sbuf("sa_t", [P, PACK], F32)
+        nc.sync.dma_start(sa_t[:], sa.rearrange("(p t) one -> p (t one)", t=PACK))
+        list5 = load_list("list5", offs5)
+        sb_t = sbuf("sb_t", [P, PACK], F32)
+        nc.sync.dma_start(sb_t[:], sb.rearrange("(p t) one -> p (t one)", t=PACK))
+        list4 = load_list("list4", offs4)
+        wb_codes = load_words(nc.sync, "wb_codes", [P, 2 * N], U8, wb_words[0])
+        for q in range(4):
+            load_scale_rows(nc.sync, wb_plane, wb_scales, q)
+
+        for q in range(4):
+            nc.vector.tensor_copy(w_plane[32 * q : 32 * q + 4, :].bitcast(I32), w_rows[:, q, :])
+        w_dealt_plane = deal(nc.gpsimd.tensor_copy, "w_dealt_plane", w_plane, U8, "p t m")
+        xg_plane = sbuf("xg_plane", [P, J], U8)
+        xg_codes = sbuf("xg_codes", [P, J], U16)
+        nc.vector.tensor_copy(xg_codes[:], xt_codes[:].indirect(list1[:]))
+        nc.vector.tensor_copy(xg_plane[:], xt_plane[:].indirect(list1[:]))
+
+        w_dealt = deal(nc.scalar.copy, "w_dealt", w_codes, U32, "p m t")
+        w2_dealt = deal(nc.gpsimd.tensor_copy, "w2_dealt", w2_codes, U32, "p t m")
+
+        def product(bank, codes, plane, dtype, t):
+            nc.tensor.matmul_mx(
+                out=bank,
+                lhsT=codes[:, t, :].bitcast(dtype),
+                lhsT_scale=plane[:, t, :],
+                rhs=xg_codes[:].bitcast(E2M1),
+                rhs_scale=xg_plane[:],
+                start=True,
+                stop=True,
+            )
+
+        a_banks = [psum.tile([P, J], F32, name=f"a_bank{t}") for t in range(PACK)]
+        for t in range(PACK):
+            product(a_banks[t][:], w_dealt, w_dealt_plane, E4M3, t)
+
+        w2_dealt_plane = deal(nc.gpsimd.tensor_copy, "w2_dealt_plane", w2_plane, U8, "p t m")
+        b_banks = [psum.tile([P, 2, J], F32, name=f"b_bank{u}") for u in range(2)]
+        for t in range(PACK):
+            product(b_banks[t // 2][:, t % 2, :], w2_dealt, w2_dealt_plane, E5M2, t)
+
+        a_rows = [sbuf(f"a_rows{t}", [P, J], F32) for t in range(PACK)]
+        split = 16 * SCALAR_COLUMNS
+        for t in range(PACK):
+            if t % 2 == 0:
+                nc.vector.tensor_copy(a_rows[t][:], a_banks[t][:])
+                nc.vector.tensor_copy(boards[t][:].indirect(list2[:]), a_rows[t][:])
+            else:
+                nc.scalar.activation(a_rows[t][:], a_banks[t][:], ACT.Copy)
+                if t < PACK - 1:
+                    nc.scalar.activation(boards[t][:].indirect(list2[:]), a_rows[t][:], ACT.Copy)
+                else:
+                    nc.scalar.activation(boards[t][:].indirect(list2[:, :SCALAR_COLUMNS]), a_rows[t][:, :split], ACT.Copy)
+                    nc.vector.tensor_copy(boards[t][:].indirect(list2[:, SCALAR_COLUMNS:]), a_rows[t][:, split:])
+
+        diff = sbuf("diff", [P, PACK, O], F32)
+        for t in range(PACK):
+            looked = sbuf(f"looked{t}", [P, J], F32)
+            nc.scalar.activation(looked[:], boards[t][:].indirect(list3[:]), ACT.Copy, scale=sa_t[:, t : t + 1])
+            rb = sbuf(f"rb{t}", [P, J], F32)
+            nc.vector.tensor_tensor(rb[:], looked[:], b_banks[t // 2][:, t % 2, :], ALU.max)
+            second = sbuf(f"second{t}", [P, O], F32)
+            nc.scalar.activation(second[:], rb[:].indirect(list5[:]), ACT.Copy, scale=sb_t[:, t : t + 1])
+            nc.vector.tensor_tensor(diff[:, t, :], rb[:].indirect(list4[:]), second[:], ALU.subtract)
+
+        hid = sbuf("hid", [P, O, PACK], BF16)
+        for t0 in (0, 2):
+            nc.scalar.activation(
+                hid[:, :, t0 : t0 + 2],
+                diff[:, t0 : t0 + 2, :].rearrange("p t o -> p o t"),
+                ACT.Abs,
+            )
+        hid_codes = sbuf("hid_codes", [P, O], U32)
+        hid_plane = sbuf("hid_plane", [P, O], U8)
+        nc.vector.quantize_mx(
+            out=hid_codes[:].bitcast(E5M2),
+            scales=hid_plane[:],
+            in_=hid[:].rearrange("p o t -> p (o t)"),
+        )
+
+        for h in range(N // P):
+            bank = psum.tile([P, O], F32, name=f"y_bank{h}")
+            nc.tensor.matmul_mx(
+                out=bank[:],
+                lhsT=wb_codes[:, 2 * P * h : 2 * P * (h + 1)].bitcast(E2M1),
+                lhsT_scale=wb_plane[:, P * h : P * (h + 1)],
+                rhs=hid_codes[:].bitcast(E5M2),
+                rhs_scale=hid_plane[:],
+                start=True,
+                stop=True,
+            )
+            y = sbuf(f"y{h}", [P, O], F32)
+            if h == 0:
+                nc.scalar.copy(y[:], bank[:])
+                nc.scalar.dma_start(out[P * h : P * (h + 1), :], y[:])
+            else:
+                nc.vector.tensor_copy(y[:], bank[:])
+                nc.sync.dma_start(out[P * h : P * (h + 1), :], y[:])

@@ -19,7 +19,7 @@ ALU = mybir.AluOpType
 
 P = 128
 PACK = 4
-SCALAR_COLUMNS = 12
+SCALAR_COLUMNS = 4
 
 
 def tile_list_boardanswer_twow_one_plain_kernel(
@@ -31,8 +31,8 @@ def tile_list_boardanswer_twow_one_plain_kernel(
         keep = ctx.enter_context(tc.tile_pool(name="keep", bufs=1))
         psum = ctx.enter_context(tc.psum_pool(name="psum", bufs=1))
 
-        def sbuf(name, shape, dtype):
-            return keep.tile(shape, dtype, name=name, align_bytes=64)
+        def sbuf(name, shape, dtype, tag=None):
+            return keep.tile(shape, dtype, name=name, tag=tag or name, align_bytes=64)
 
         def load_list(name, src):
             dst = sbuf(name, list(src.shape), U16)
@@ -57,11 +57,11 @@ def tile_list_boardanswer_twow_one_plain_kernel(
 
         def deal(copy, name, src, dtype, order):
             dst = sbuf(name, [P, PACK, P], dtype)
-            copy(dst[:].rearrange(f"p t m -> {order}"), src[:].rearrange(f"p (m t) -> {order}", t=PACK))
+            copy(dst[:].rearrange(f"p t m -> {order}"), src.rearrange(f"p (m t) -> {order}", t=PACK))
             return dst
 
         xt_plane = zeroed_plane(nc.vector, "xt_plane", T)
-        w_plane = zeroed_plane(nc.vector, "w_plane", R)
+        w_plane = zeroed_plane(nc.vector, "w_plane", 2 * R)
 
         w_rows = sbuf("w_rows", [4, 4, R // 4], I32)
         nc.sync.dma_start(w_rows[:], w_scales[0].bitcast(I32).rearrange("(q r) c -> r q c", r=4))
@@ -70,7 +70,6 @@ def tile_list_boardanswer_twow_one_plain_kernel(
         w_codes = load_words(nc.scalar, "w_codes", [P, R], U32, w_words[0].rearrange("p n t -> p (n t)"))
         for q in range(4):
             load_scale_rows(nc.sync, xt_plane, xt_scales, q)
-        list2 = load_list("list2", offs2)
 
         w2_plane = zeroed_plane(nc.gpsimd, "w2_plane", R)
         wb_plane = zeroed_plane(nc.gpsimd, "wb_plane", N)
@@ -81,6 +80,7 @@ def tile_list_boardanswer_twow_one_plain_kernel(
             boards.append(board)
 
         w2_codes = load_words(nc.sync, "w2_codes", [P, R], U32, w2_words[0].rearrange("p n t -> p (n t)"))
+        list2 = load_list("list2", offs2)
         for q in range(4):
             load_scale_rows(nc.sync, w2_plane, w2_scales, q)
         list3 = load_list("list3", offs3)
@@ -94,16 +94,23 @@ def tile_list_boardanswer_twow_one_plain_kernel(
         for q in range(4):
             load_scale_rows(nc.sync, wb_plane, wb_scales, q)
 
-        for q in range(4):
-            nc.vector.tensor_copy(w_plane[32 * q : 32 * q + 4, :].bitcast(I32), w_rows[:, q, :])
-        w_dealt_plane = deal(nc.gpsimd.tensor_copy, "w_dealt_plane", w_plane, U8, "p t m")
+        w_halves = w_plane[:].bitcast(I32).rearrange("p (h c) -> p h c", h=2)
+        for q in range(2):
+            nc.vector.tensor_copy(w_halves[32 * q : 32 * q + 4], w_rows[:, q::2, :])
+        nc.vector.tensor_copy(w_halves[64:128, 0, :], w_halves[0:64, 1, :])
+        w_dealt_plane = deal(nc.gpsimd.tensor_copy, "w_dealt_plane", w_plane[:, :R], U8, "p t m")
         xg_plane = sbuf("xg_plane", [P, J], U8)
         xg_codes = sbuf("xg_codes", [P, J], U16)
         nc.vector.tensor_copy(xg_codes[:], xt_codes[:].indirect(list1[:]))
         nc.vector.tensor_copy(xg_plane[:], xt_plane[:].indirect(list1[:]))
 
-        w_dealt = deal(nc.scalar.copy, "w_dealt", w_codes, U32, "p m t")
-        w2_dealt = deal(nc.gpsimd.tensor_copy, "w2_dealt", w2_codes, U32, "p t m")
+        w_dealt = sbuf("w_dealt", [P, PACK, P], U32)
+        for t0 in (0, 2):
+            nc.scalar.copy(
+                w_dealt[:, t0 : t0 + 2, :].rearrange("p t m -> p m t"),
+                w_codes[:].rearrange("p (m t) -> p m t", t=PACK)[:, :, t0 : t0 + 2],
+            )
+        w2_dealt = deal(nc.scalar.copy, "w2_dealt", w2_codes[:], U32, "p m t")
 
         def product(bank, codes, plane, dtype, t):
             nc.tensor.matmul_mx(
@@ -120,34 +127,40 @@ def tile_list_boardanswer_twow_one_plain_kernel(
         for t in range(PACK):
             product(a_banks[t][:], w_dealt, w_dealt_plane, E4M3, t)
 
-        w2_dealt_plane = deal(nc.gpsimd.tensor_copy, "w2_dealt_plane", w2_plane, U8, "p t m")
+        w2_dealt_plane = deal(nc.gpsimd.tensor_copy, "w2_dealt_plane", w2_plane[:], U8, "p t m")
         b_banks = [psum.tile([P, 2, J], F32, name=f"b_bank{u}") for u in range(2)]
         for t in range(PACK):
             product(b_banks[t // 2][:, t % 2, :], w2_dealt, w2_dealt_plane, E5M2, t)
 
-        a_rows = [sbuf(f"a_rows{t}", [P, J], F32) for t in range(PACK)]
+        a_first = sbuf("a_first", [P, J], F32)
+        a_others = sbuf("a_others", [P, PACK - 1, J], F32, "w2_codes")
+        a_rows = [a_first[:]] + [a_others[:, t, :] for t in range(PACK - 1)]
+        nc.vector.tensor_copy(a_rows[0], a_banks[0][:])
+        for t in range(1, PACK):
+            nc.scalar.activation(a_rows[t], a_banks[t][:], ACT.Copy)
         split = 16 * SCALAR_COLUMNS
-        for t in range(PACK):
-            if t % 2 == 0:
-                nc.vector.tensor_copy(a_rows[t][:], a_banks[t][:])
-                nc.vector.tensor_copy(boards[t][:].indirect(list2[:]), a_rows[t][:])
-            else:
-                nc.scalar.activation(a_rows[t][:], a_banks[t][:], ACT.Copy)
-                if t < PACK - 1:
-                    nc.scalar.activation(boards[t][:].indirect(list2[:]), a_rows[t][:], ACT.Copy)
-                else:
-                    nc.scalar.activation(boards[t][:].indirect(list2[:, :SCALAR_COLUMNS]), a_rows[t][:, :split], ACT.Copy)
-                    nc.vector.tensor_copy(boards[t][:].indirect(list2[:, SCALAR_COLUMNS:]), a_rows[t][:, split:])
+        last = PACK - 1
+        nc.vector.tensor_copy(boards[0][:].indirect(list2[:]), a_rows[0])
+        nc.scalar.activation(boards[1][:].indirect(list2[:]), a_rows[1], ACT.Copy)
+        nc.vector.tensor_copy(boards[2][:].indirect(list2[:]), a_rows[2])
+        nc.scalar.activation(boards[last][:].indirect(list2[:, :SCALAR_COLUMNS]), a_rows[last][:, :split], ACT.Copy)
+        nc.vector.tensor_copy(boards[last][:].indirect(list2[:, SCALAR_COLUMNS:]), a_rows[last][:, split:])
 
+        looked = [sbuf(f"looked{t}", [P, J], F32) for t in range(PACK)]
+        rb = [sbuf(f"rb{t}", [P, J], F32) for t in range(PACK)]
+        second = [sbuf(f"second{t}", [P, O], F32) for t in range(PACK)]
         diff = sbuf("diff", [P, PACK, O], F32)
         for t in range(PACK):
-            looked = sbuf(f"looked{t}", [P, J], F32)
-            nc.scalar.activation(looked[:], boards[t][:].indirect(list3[:]), ACT.Copy, scale=sa_t[:, t : t + 1])
-            rb = sbuf(f"rb{t}", [P, J], F32)
-            nc.vector.tensor_tensor(rb[:], looked[:], b_banks[t // 2][:, t % 2, :], ALU.max)
-            second = sbuf(f"second{t}", [P, O], F32)
-            nc.scalar.activation(second[:], rb[:].indirect(list5[:]), ACT.Copy, scale=sb_t[:, t : t + 1])
-            nc.vector.tensor_tensor(diff[:, t, :], rb[:].indirect(list4[:]), second[:], ALU.subtract)
+            nc.scalar.activation(looked[t][:], boards[t][:].indirect(list3[:]), ACT.Copy, scale=sa_t[:, t : t + 1])
+        for t in range(PACK):
+            nc.vector.tensor_tensor(rb[t][:], looked[t][:], b_banks[t // 2][:, t % 2, :], ALU.max)
+        for t in range(PACK):
+            nc.scalar.activation(second[t][:], rb[t][:].indirect(list5[:]), ACT.Copy, scale=sb_t[:, t : t + 1])
+        for t in range(last):
+            nc.vector.tensor_tensor(diff[:, t, :], rb[t][:].indirect(list4[:]), second[t][:], ALU.subtract)
+        first = sbuf("first", [P, O], F32)
+        nc.scalar.activation(first[:], rb[last][:].indirect(list4[:]), ACT.Copy)
+        nc.vector.tensor_tensor(diff[:, last, :], first[:], second[last][:], ALU.subtract)
 
         hid = sbuf("hid", [P, O, PACK], BF16)
         for t0 in (0, 2):

@@ -19,7 +19,7 @@ ALU = mybir.AluOpType
 
 P = 128
 PACK = 4
-SCALAR_COLUMNS = 4
+SCALAR_COLUMNS = 6
 
 
 def tile_list_boardanswer_twow_one_plain_kernel(
@@ -79,8 +79,8 @@ def tile_list_boardanswer_twow_one_plain_kernel(
             (nc.vector if t % 2 == 0 else nc.gpsimd).memset(board[:], 0.0)
             boards.append(board)
 
-        w2_codes = load_words(nc.sync, "w2_codes", [P, R], U32, w2_words[0].rearrange("p n t -> p (n t)"))
         list2 = load_list("list2", offs2)
+        w2_codes = load_words(nc.sync, "w2_codes", [P, R], U32, w2_words[0].rearrange("p n t -> p (n t)"))
         for q in range(4):
             load_scale_rows(nc.sync, w2_plane, w2_scales, q)
         list3 = load_list("list3", offs3)
@@ -102,7 +102,10 @@ def tile_list_boardanswer_twow_one_plain_kernel(
         xg_plane = sbuf("xg_plane", [P, J], U8)
         xg_codes = sbuf("xg_codes", [P, J], U16)
         nc.vector.tensor_copy(xg_codes[:], xt_codes[:].indirect(list1[:]))
-        nc.vector.tensor_copy(xg_plane[:], xt_plane[:].indirect(list1[:]))
+        half = J // 2
+        halves = [(slice(0, half), slice(0, half // 16)), (slice(half, J), slice(half // 16, J // 16))]
+        for slots, columns in halves:
+            nc.vector.tensor_copy(xg_plane[:, slots], xt_plane[:].indirect(list1[:, columns]))
 
         w_dealt = sbuf("w_dealt", [P, PACK, P], U32)
         for t0 in (0, 2):
@@ -110,38 +113,44 @@ def tile_list_boardanswer_twow_one_plain_kernel(
                 w_dealt[:, t0 : t0 + 2, :].rearrange("p t m -> p m t"),
                 w_codes[:].rearrange("p (m t) -> p m t", t=PACK)[:, :, t0 : t0 + 2],
             )
-        w2_dealt = deal(nc.scalar.copy, "w2_dealt", w2_codes[:], U32, "p m t")
+        w2_dealt = deal(nc.gpsimd.tensor_copy, "w2_dealt", w2_codes[:], U32, "p t m")
 
-        def product(bank, codes, plane, dtype, t):
+        def product(bank, codes, plane, dtype, t, slots):
             nc.tensor.matmul_mx(
                 out=bank,
                 lhsT=codes[:, t, :].bitcast(dtype),
                 lhsT_scale=plane[:, t, :],
-                rhs=xg_codes[:].bitcast(E2M1),
-                rhs_scale=xg_plane[:],
+                rhs=xg_codes[:, slots].bitcast(E2M1),
+                rhs_scale=xg_plane[:, slots],
                 start=True,
                 stop=True,
             )
 
-        a_banks = [psum.tile([P, J], F32, name=f"a_bank{t}") for t in range(PACK)]
-        for t in range(PACK):
-            product(a_banks[t][:], w_dealt, w_dealt_plane, E4M3, t)
+        a_banks = {}
+        for u, (slots, columns) in enumerate(halves):
+            for t in range(2):
+                a_banks[t, u] = psum.tile([P, half], F32, name=f"a_bank{t}{u}")
+                product(a_banks[t, u][:], w_dealt, w_dealt_plane, E4M3, t, slots)
+        for t in range(2, PACK):
+            a_banks[t] = psum.tile([P, J], F32, name=f"a_bank{t}")
+            product(a_banks[t][:], w_dealt, w_dealt_plane, E4M3, t, slice(0, J))
 
         w2_dealt_plane = deal(nc.gpsimd.tensor_copy, "w2_dealt_plane", w2_plane[:], U8, "p t m")
         b_banks = [psum.tile([P, 2, J], F32, name=f"b_bank{u}") for u in range(2)]
         for t in range(PACK):
-            product(b_banks[t // 2][:, t % 2, :], w2_dealt, w2_dealt_plane, E5M2, t)
+            product(b_banks[t // 2][:, t % 2, :], w2_dealt, w2_dealt_plane, E5M2, t, slice(0, J))
 
-        a_first = sbuf("a_first", [P, J], F32)
-        a_others = sbuf("a_others", [P, PACK - 1, J], F32, "w2_codes")
-        a_rows = [a_first[:]] + [a_others[:, t, :] for t in range(PACK - 1)]
-        nc.vector.tensor_copy(a_rows[0], a_banks[0][:])
-        for t in range(1, PACK):
-            nc.scalar.activation(a_rows[t], a_banks[t][:], ACT.Copy)
+        a_rows = [sbuf(f"a_rows{t}", [P, J], F32)[:] for t in range(PACK)]
+        for u, (slots, columns) in enumerate(halves):
+            nc.vector.tensor_copy(a_rows[0][:, slots], a_banks[0, u][:])
+            nc.vector.tensor_copy(boards[0][:].indirect(list2[:, columns]), a_rows[0][:, slots])
+            nc.scalar.activation(a_rows[1][:, slots], a_banks[1, u][:], ACT.Copy)
+            if u == 1:
+                for t in range(2, PACK):
+                    nc.scalar.activation(a_rows[t], a_banks[t][:], ACT.Copy)
+            nc.scalar.activation(boards[1][:].indirect(list2[:, columns]), a_rows[1][:, slots], ACT.Copy)
         split = 16 * SCALAR_COLUMNS
         last = PACK - 1
-        nc.vector.tensor_copy(boards[0][:].indirect(list2[:]), a_rows[0])
-        nc.scalar.activation(boards[1][:].indirect(list2[:]), a_rows[1], ACT.Copy)
         nc.vector.tensor_copy(boards[2][:].indirect(list2[:]), a_rows[2])
         nc.scalar.activation(boards[last][:].indirect(list2[:, :SCALAR_COLUMNS]), a_rows[last][:, :split], ACT.Copy)
         nc.vector.tensor_copy(boards[last][:].indirect(list2[:, SCALAR_COLUMNS:]), a_rows[last][:, split:])
@@ -163,12 +172,12 @@ def tile_list_boardanswer_twow_one_plain_kernel(
         nc.vector.tensor_tensor(diff[:, last, :], first[:], second[last][:], ALU.subtract)
 
         hid = sbuf("hid", [P, O, PACK], BF16)
-        for t0 in (0, 2):
-            nc.scalar.activation(
-                hid[:, :, t0 : t0 + 2],
-                diff[:, t0 : t0 + 2, :].rearrange("p t o -> p o t"),
-                ACT.Abs,
-            )
+        by_place = diff[:].rearrange("p t o -> p o t")
+        nc.scalar.activation(hid[:, :, 0:2], by_place[:, :, 0:2], ACT.Abs)
+        nc.scalar.activation(hid[:, : O // 2, 2:4], by_place[:, : O // 2, 2:4], ACT.Abs)
+        nc.vector.scalar_tensor_tensor(
+            hid[:, O // 2 :, 2:4], by_place[:, O // 2 :, 2:4], -1.0, by_place[:, O // 2 :, 2:4], ALU.mult, ALU.max
+        )
         hid_codes = sbuf("hid_codes", [P, O], U32)
         hid_plane = sbuf("hid_plane", [P, O], U8)
         nc.vector.quantize_mx(
@@ -178,7 +187,7 @@ def tile_list_boardanswer_twow_one_plain_kernel(
         )
 
         for h in range(N // P):
-            bank = psum.tile([P, O], F32, name=f"y_bank{h}")
+            bank = psum.tile([P, O], F32, name=f"y_bank{h}", tag=f"a_bank{h}0")
             nc.tensor.matmul_mx(
                 out=bank[:],
                 lhsT=wb_codes[:, 2 * P * h : 2 * P * (h + 1)].bitcast(E2M1),

from contextlib import ExitStack

import concourse.mybir as mybir

K, T, J, R, C, O, N = 512, 1024, 256, 512, 512, 128, 256
FLOPS = 2 * K * R * J * 2 + 2 * R * N * O

F32 = mybir.dt.float32
BF16 = mybir.dt.bfloat16
I32 = mybir.dt.int32
U32 = mybir.dt.uint32
U16 = mybir.dt.uint16
U8 = mybir.dt.uint8
E4M3 = mybir.dt.float8_e4m3fn_x4
E5M2 = mybir.dt.float8_e5m2_x4
E2M1 = mybir.dt.float4_e2m1fn_x4
ACT = mybir.ActivationFunctionType
ALU = mybir.AluOpType

P = 128
PACK = 4
SCALAR_COLUMNS = 6


def tile_list_boardanswer_twow_one_plain_kernel(
    tc, xt_words, xt_scales, w_words, w_scales, w2_words, w2_scales, sa, sb,
    wb_words, wb_scales, offs, offs2, offs3, offs4, offs5, out,
):
    nc = tc.nc
    with ExitStack() as ctx:
        keep = ctx.enter_context(tc.tile_pool(name="keep", bufs=1))
        psum = ctx.enter_context(tc.psum_pool(name="psum", bufs=1))

        def sbuf(name, shape, dtype, tag=None):
            return keep.tile(shape, dtype, name=name, tag=tag or name, align_bytes=64)

        def load_list(name, src):
            dst = sbuf(name, list(src.shape), U16)
            nc.sync.dma_start(dst[:], src)
            return dst

        def zeroed_plane(engine, name, width):
            plane = sbuf(name, [P, width], U8)
            engine.memset(plane[:].bitcast(I32), 0)
            return plane

        def load_scale_rows(queue, plane, src, quadrant):
            queue.dma_start(
                plane[32 * quadrant : 32 * quadrant + 4, :].bitcast(I32),
                src[0, 4 * quadrant : 4 * quadrant + 4, :].bitcast(I32),
            )

        def load_words(queue, name, shape, dtype, src):
            dst = sbuf(name, shape, dtype)
            queue.dma_start(dst[:].bitcast(I32), src.bitcast(I32))
            return dst

        def deal(copy, name, src, dtype, order):
            dst = sbuf(name, [P, PACK, P], dtype)
            copy(dst[:].rearrange(f"p t m -> {order}"), src.rearrange(f"p (m t) -> {order}", t=PACK))
            return dst

        xt_plane = zeroed_plane(nc.vector, "xt_plane", T)
        w_plane = zeroed_plane(nc.vector, "w_plane", 2 * R)

        w_rows = sbuf("w_rows", [4, 4, R // 4], I32)
        nc.sync.dma_start(w_rows[:], w_scales[0].bitcast(I32).rearrange("(q r) c -> r q c", r=4))
        list1 = load_list("list1", offs)
        xt_codes = load_words(nc.scalar, "xt_codes", [P, T], U16, xt_words[0])
        w_codes = load_words(nc.scalar, "w_codes", [P, R], U32, w_words[0].rearrange("p n t -> p (n t)"))
        for q in range(4):
            load_scale_rows(nc.sync, xt_plane, xt_scales, q)

        w2_plane = zeroed_plane(nc.gpsimd, "w2_plane", R)
        wb_plane = zeroed_plane(nc.gpsimd, "wb_plane", N)
        boards = []
        for t in range(PACK):
            board = sbuf(f"board{t}", [P, C], F32)
            (nc.vector if t % 2 == 0 else nc.gpsimd).memset(board[:], 0.0)
            boards.append(board)

        list2 = load_list("list2", offs2)
        w2_codes = load_words(nc.sync, "w2_codes", [P, R], U32, w2_words[0].rearrange("p n t -> p (n t)"))
        for q in range(4):
            load_scale_rows(nc.sync, w2_plane, w2_scales, q)
        list3 = load_list("list3", offs3)
        sa_t = sbuf("sa_t", [P, PACK], F32)
        nc.sync.dma_start(sa_t[:], sa.rearrange("(p t) one -> p (t one)", t=PACK))
        list5 = load_list("list5", offs5)
        sb_t = sbuf("sb_t", [P, PACK], F32)
        nc.sync.dma_start(sb_t[:], sb.rearrange("(p t) one -> p (t one)", t=PACK))
        list4 = load_list("list4", offs4)
        wb_codes = load_words(nc.sync, "wb_codes", [P, 2 * N], U8, wb_words[0])
        for q in range(4):
            load_scale_rows(nc.sync, wb_plane, wb_scales, q)

        w_halves = w_plane[:].bitcast(I32).rearrange("p (h c) -> p h c", h=2)
        for q in range(2):
            nc.vector.tensor_copy(w_halves[32 * q : 32 * q + 4], w_rows[:, q::2, :])
        nc.vector.tensor_copy(w_halves[64:128, 0, :], w_halves[0:64, 1, :])
        w_dealt_plane = deal(nc.gpsimd.tensor_copy, "w_dealt_plane", w_plane[:, :R], U8, "p t m")
        xg_plane = sbuf("xg_plane", [P, J], U8)
        xg_codes = sbuf("xg_codes", [P, J], U16)
        nc.vector.tensor_copy(xg_codes[:], xt_codes[:].indirect(list1[:]))
        half = J // 2
        halves = [(slice(0, half), slice(0, half // 16)), (slice(half, J), slice(half // 16, J // 16))]
        for slots, columns in halves:
            nc.vector.tensor_copy(xg_plane[:, slots], xt_plane[:].indirect(list1[:, columns]))

        w_dealt = sbuf("w_dealt", [P, PACK, P], U32)
        for t0 in (0, 2):
            nc.scalar.copy(
                w_dealt[:, t0 : t0 + 2, :].rearrange("p t m -> p m t"),
                w_codes[:].rearrange("p (m t) -> p m t", t=PACK)[:, :, t0 : t0 + 2],
            )
        w2_dealt = deal(nc.gpsimd.tensor_copy, "w2_dealt", w2_codes[:], U32, "p t m")

        def product(bank, codes, plane, dtype, t, slots):
            nc.tensor.matmul_mx(
                out=bank,
                lhsT=codes[:, t, :].bitcast(dtype),
                lhsT_scale=plane[:, t, :],
                rhs=xg_codes[:, slots].bitcast(E2M1),
                rhs_scale=xg_plane[:, slots],
                start=True,
                stop=True,
            )

        a_banks = {}
        for u, (slots, columns) in enumerate(halves):
            for t in range(2):
                a_banks[t, u] = psum.tile([P, half], F32, name=f"a_bank{t}{u}")
                product(a_banks[t, u][:], w_dealt, w_dealt_plane, E4M3, t, slots)
        for t in range(2, PACK):
            a_banks[t] = psum.tile([P, J], F32, name=f"a_bank{t}")
            product(a_banks[t][:], w_dealt, w_dealt_plane, E4M3, t, slice(0, J))

        w2_dealt_plane = deal(nc.gpsimd.tensor_copy, "w2_dealt_plane", w2_plane[:], U8, "p t m")
        b_banks = [psum.tile([P, 2, J], F32, name=f"b_bank{u}") for u in range(2)]
        for t in range(PACK):
            product(b_banks[t // 2][:, t % 2, :], w2_dealt, w2_dealt_plane, E5M2, t, slice(0, J))

        a_rows = [sbuf(f"a_rows{t}", [P, J], F32)[:] for t in range(PACK)]
        for u, (slots, columns) in enumerate(halves):
            nc.vector.tensor_copy(a_rows[0][:, slots], a_banks[0, u][:])
            nc.vector.tensor_copy(boards[0][:].indirect(list2[:, columns]), a_rows[0][:, slots])
            nc.scalar.activation(a_rows[1][:, slots], a_banks[1, u][:], ACT.Copy)
            if u == 1:
                for t in range(2, PACK):
                    nc.scalar.activation(a_rows[t], a_banks[t][:], ACT.Copy)
            nc.scalar.activation(boards[1][:].indirect(list2[:, columns]), a_rows[1][:, slots], ACT.Copy)
        split = 16 * SCALAR_COLUMNS
        last = PACK - 1
        nc.vector.tensor_copy(boards[2][:].indirect(list2[:]), a_rows[2])
        nc.scalar.activation(boards[last][:].indirect(list2[:, :SCALAR_COLUMNS]), a_rows[last][:, :split], ACT.Copy)
        nc.vector.tensor_copy(boards[last][:].indirect(list2[:, SCALAR_COLUMNS:]), a_rows[last][:, split:])

        looked = [sbuf(f"looked{t}", [P, J], F32) for t in range(PACK)]
        rb = [sbuf(f"rb{t}", [P, J], F32) for t in range(PACK)]
        second = [sbuf(f"second{t}", [P, O], F32) for t in range(PACK)]
        diff = sbuf("diff", [P, PACK, O], F32)
        for t in range(PACK):
            nc.scalar.activation(looked[t][:], boards[t][:].indirect(list3[:]), ACT.Copy, scale=sa_t[:, t : t + 1])
        for t in range(PACK):
            nc.vector.tensor_tensor(rb[t][:], looked[t][:], b_banks[t // 2][:, t % 2, :], ALU.max)
        for t in range(PACK):
            nc.scalar.activation(second[t][:], rb[t][:].indirect(list5[:]), ACT.Copy, scale=sb_t[:, t : t + 1])
        for t in range(last):
            nc.vector.tensor_tensor(diff[:, t, :], rb[t][:].indirect(list4[:]), second[t][:], ALU.subtract)
        first = sbuf("first", [P, O], F32)
        nc.scalar.activation(first[:], rb[last][:].indirect(list4[:]), ACT.Copy)
        nc.vector.tensor_tensor(diff[:, last, :], first[:], second[last][:], ALU.subtract)

        hid = sbuf("hid", [P, O, PACK], BF16)
        by_place = diff[:].rearrange("p t o -> p o t")
        nc.scalar.activation(hid[:, :, 0:2], by_place[:, :, 0:2], ACT.Abs)
        nc.scalar.activation(hid[:, : O // 2, 2:4], by_place[:, : O // 2, 2:4], ACT.Abs)
        nc.vector.scalar_tensor_tensor(
            hid[:, O // 2 :, 2:4], by_place[:, O // 2 :, 2:4], -1.0, by_place[:, O // 2 :, 2:4], ALU.mult, ALU.max
        )
        hid_codes = sbuf("hid_codes", [P, O], U32)
        hid_plane = sbuf("hid_plane", [P, O], U8)
        nc.vector.quantize_mx(
            out=hid_codes[:].bitcast(E5M2),
            scales=hid_plane[:],
            in_=hid[:].rearrange("p o t -> p (o t)"),
        )

        for h in range(N // P):
            bank = psum.tile([P, O], F32, name=f"y_bank{h}", tag=f"a_bank{h}0")
            nc.tensor.matmul_mx(
                out=bank[:],
                lhsT=wb_codes[:, 2 * P * h : 2 * P * (h + 1)].bitcast(E2M1),
                lhsT_scale=wb_plane[:, P * h : P * (h + 1)],
                rhs=hid_codes[:].bitcast(E5M2),
                rhs_scale=hid_plane[:],
                start=True,
                stop=True,
            )
            y = sbuf(f"y{h}", [P, O], F32)
            if h == 0:
                nc.scalar.copy(y[:], bank[:])
                nc.scalar.dma_start(out[P * h : P * (h + 1), :], y[:])
            else:
                nc.vector.tensor_copy(y[:], bank[:])
                nc.sync.dma_start(out[P * h : P * (h + 1), :], y[:])
